import numpy as np
import ml_dtypes


def mxq(x, axis, fmt="e4m3"):
    dtype, down = {"e4m3": (ml_dtypes.float8_e4m3fn, 7), "e5m2": (ml_dtypes.float8_e5m2, 14)}[fmt]
    v = np.moveaxis(np.asarray(x, np.float32).astype(ml_dtypes.bfloat16).astype(np.float64), axis, -1)
    blocks = v.reshape(v.shape[:-1] + (-1, 32))
    amax = np.abs(blocks).max(-1, keepdims=True)
    byte = np.maximum(np.where(amax > 0, np.frexp(amax)[1] - 1 + 127, 0) - down, 1)
    scale = np.exp2(byte - 127.0)
    codes = (blocks / scale).astype(np.float32).astype(dtype).astype(np.float64)
    return np.moveaxis((codes * scale).reshape(v.shape), -1, axis)


WIDE = False


def mx_kscale(k):
    if not WIDE:
        return np.ones(k)
    levels = np.array([10, -10, 5, -5, 0])
    if k % 512:
        return np.exp2(np.random.permutation(np.resize(levels, k // 32))).repeat(32)
    a = np.empty((k // 512, 16))
    for p in range(k // 512):
        a[p, :8] = np.random.permutation(np.resize(levels, 8))
        for g in range(8):
            far = levels[np.abs(levels - a[p, g]) >= 10]
            a[p, g + 8] = far[np.random.randint(len(far))]
    return np.exp2(a.ravel()).repeat(32)


def f64(x):
    return np.asarray(x).astype(np.float64)


def striped8(idx):
    return np.asarray(idx).reshape(8, -1, 16).transpose(0, 2, 1).reshape(128, -1).astype(np.uint16)


def unstriped8(offs):
    return offs.reshape(8, 16, -1).transpose(0, 2, 1).reshape(8, -1).astype(np.int64)


def pick8(x, idx, run):
    r = np.arange(len(x))
    return x[r[:, None], idx[r % (8 * run) // run]]


E2M1 = np.array([0.0, 0.5, 1.0, 1.5, 2.0, 3.0, 4.0, 6.0, -0.0, -0.5, -1.0, -1.5, -2.0, -3.0, -4.0, -6.0])


def pack_weight(w, fmt):
    k, n = w.shape
    w = f64(np.asarray(w, np.float32).astype(ml_dtypes.bfloat16)).reshape(k // 32, 32, n)
    amax = np.abs(w).max(1)
    if fmt == "e4m3":
        byte = np.frexp(amax)[1] - 1 + 127 - 7
    else:
        mant, ex = np.frexp(amax / 6.0)
        byte = np.where(mant > 0.5, ex, ex - 1) + 127
    byte = np.clip(np.where(amax > 0, byte, 1), 1, 254)
    scaled = (w * np.exp2(127.0 - byte)[:, None, :]).reshape(k, n).astype(np.float32)
    by_word = np.ascontiguousarray(scaled.reshape(k // 512, 128, 4, n).transpose(0, 1, 3, 2))
    if fmt == "e4m3":
        words = by_word.astype(ml_dtypes.float8_e4m3fn).view(np.uint8)
    else:
        c = by_word.astype(ml_dtypes.float4_e2m1fn).view(np.uint8) & 0xF
        words = (c[..., 0::2] | (c[..., 1::2] << 4)).reshape(k // 512, 128, 2 * n)
    return np.ascontiguousarray(words), np.ascontiguousarray(byte.astype(np.uint8).reshape(k // 512, 16, n))


def unpack_weight(words, scales, fmt):
    g, _, n = scales.shape
    words = np.ascontiguousarray(words).reshape(g, 128, n, -1)
    if fmt == "e4m3":
        vals = words.view(ml_dtypes.float8_e4m3fn).astype(np.float64)
    else:
        nib = np.empty((g, 128, n, 4), np.uint8)
        nib[..., 0::2] = words & 0xF
        nib[..., 1::2] = words >> 4
        vals = E2M1[nib]
    vals = vals * np.repeat(np.exp2(scales.astype(np.float64) - 127.0), 8, axis=1)[..., None]
    return vals.transpose(0, 1, 3, 2).reshape(g * 512, n)


D, T, I, Q = 512, 1024, 512, 128


def setup_inputs():
    n = np.random.standard_normal
    idx = np.stack([np.random.permutation(T)[:I] for _ in range(8)])
    idx2 = np.stack([np.random.permutation(T)[:I] for _ in range(8)])
    idx3 = np.stack([np.random.permutation(T)[:I] for _ in range(8)])
    fd = mx_kscale(D)
    keysp = pack_weight(n((D, T)) / fd[:, None], "e2m1")
    return {
        "query": (n((D, Q)) * 0.9 / np.sqrt(D) * fd[:, None]).astype(np.float32),
        "query2": (n((D, Q)) * 0.9 / np.sqrt(D) * fd[:, None]).astype(np.float32),
        "keys_words": keysp[0],
        "keys_scales": keysp[1],
        "lam": (np.random.uniform(0.5, 1.3, (Q, 1))).astype(np.float32),
        "old": (1.0 * n((Q, T))).astype(np.float32),
        "offs": striped8(idx),
        "offs2": striped8(idx2),
        "offs3": striped8(idx3),
    }


def reference(query, query2, keys_words, keys_scales, lam, old, offs, offs2, offs3):
    idx = unstriped8(offs)
    idx2 = unstriped8(offs2)
    idx3 = unstriped8(offs3)
    keysu = unpack_weight(keys_words, keys_scales, "e2m1")
    queryq = mxq(f64(query), 0, "e4m3")
    a = queryq.T @ keysu
    query2q = mxq(f64(query2), 0, "e4m3")
    b = query2q.T @ keysu
    w = (np.maximum(pick8(a, idx, 16), pick8(b, idx2, 16)) - np.maximum(pick8(a, idx2, 16), pick8(b, idx, 16))) * f64(lam)
    f1 = np.zeros((Q, T))
    f1[np.arange(Q)[:, None], idx3[np.arange(Q) % 128 // 16]] = w
    y = f64(old) + f1
    return y

@@ -1,0 +1,115 @@
+from contextlib import ExitStack
+
+import concourse.mybir as mybir
+
+D, T, I, Q = 512, 1024, 512, 128
+FLOPS = 2 * 2 * D * T * Q
+
+F32 = mybir.dt.float32
+BF16 = mybir.dt.bfloat16
+I32 = mybir.dt.int32
+U32 = mybir.dt.uint32
+U16 = mybir.dt.uint16
+U8 = mybir.dt.uint8
+FP8X4 = mybir.dt.float8_e4m3fn_x4
+FP4X4 = mybir.dt.float4_e2m1fn_x4
+ALU = mybir.AluOpType
+COPY = mybir.ActivationFunctionType.Copy
+
+P = 128
+PACK = 4
+PIECE = 256
+CHUNK = 256
+STORE = 256
+
+
+def tile_attend_exchanged_lean_putold_heads_kernel(tc, query, query2, keys_words, keys_scales, lam, old, offs, offs2, offs3, out):
+    nc = tc.nc
+    with ExitStack() as ctx:
+        sb = ctx.enter_context(tc.tile_pool(name="sb", bufs=1))
+        ps = ctx.enter_context(tc.psum_pool(name="ps", bufs=1))
+
+        list1 = sb.tile([P, I // 16], U16, name="list1")
+        list2 = sb.tile([P, I // 16], U16, name="list2")
+        list3 = sb.tile([P, I // 16], U16, name="list3")
+        stage = sb.tile([P, T], F32, name="stage")
+        words = sb.tile([P, 2 * T], U8, name="words", align_bytes=64)
+        kscale = sb.tile([P, T], U8, name="kscale", align_bytes=64)
+        lam_col = sb.tile([P, 1], F32, name="lam_col")
+        placed = sb.tile([P, T], F32, name="placed")
+
+        nc.vector.memset(placed[:], 0.0)
+        words_hbm = keys_words[0].bitcast(I32)
+        scales_hbm = keys_scales[0].bitcast(I32)
+        nc.sync.dma_start(out=stage[:, 0:512], in_=query.rearrange("(p j) q -> p (j q)", j=PACK))
+        nc.scalar.dma_start(out=lam_col[:], in_=lam)
+        for quad in range(4):
+            nc.sync.dma_start(out=kscale[32 * quad : 32 * quad + 4, :].bitcast(I32), in_=scales_hbm[4 * quad : 4 * quad + 4, :])
+        nc.sync.dma_start(out=words[:].bitcast(I32), in_=words_hbm)
+        nc.sync.dma_start(out=stage[:, 512:1024], in_=query2.rearrange("(p j) q -> p (j q)", j=PACK))
+        nc.sync.dma_start(list1[:], offs)
+        nc.sync.dma_start(list2[:], offs2)
+        nc.sync.dma_start(list3[:], offs3)
+
+        scores = [sb.tile([P, T], F32, name="scores%d" % s) for s in range(2)]
+        for s in range(2):
+            grouped = sb.tile([P, Q, PACK], BF16, name="grouped%d" % s, align_bytes=64)
+            src = stage[:, 512 * s : 512 * (s + 1)].rearrange("p (j c i) -> p c j i", j=PACK, i=4)
+            dst = grouped[:].rearrange("p (c i) j -> p c j i", i=4)
+            nc.vector.tensor_copy(out=dst, in_=src)
+            codes = sb.tile([P, Q], U32, name="codes%d" % s, align_bytes=64)
+            qscale = sb.tile([P, Q], U8, name="qscale%d" % s, align_bytes=64)
+            nc.vector.quantize_mx(out=codes[:].bitcast(FP8X4), scales=qscale[:], in_=grouped[:].rearrange("p q j -> p (q j)"))
+            for n in range(T // PIECE):
+                bank = ps.tile([P, PIECE], F32, name="bank%d_%d" % (s, n))
+                nc.tensor.matmul_mx(
+                    out=bank[:],
+                    lhsT=codes[:].bitcast(FP8X4),
+                    lhsT_scale=qscale[:],
+                    rhs=words[:, 2 * n * PIECE : 2 * (n + 1) * PIECE].bitcast(FP4X4),
+                    rhs_scale=kscale[:, n * PIECE : (n + 1) * PIECE],
+                    start=True,
+                    stop=True,
+                )
+                if s == 0:
+                    nc.scalar.activation(out=scores[s][:, n * PIECE : (n + 1) * PIECE], in_=bank[:], func=COPY)
+                else:
+                    nc.vector.tensor_copy(out=scores[s][:, n * PIECE : (n + 1) * PIECE], in_=bank[:])
+
+        nc.sync.dma_start(out=stage[:], in_=old)
+        lam_wide = sb.tile([P, CHUNK], F32, name="lam_wide")
+        nc.scalar.activation(out=lam_wide[:], in_=lam_col[:, 0:1].to_broadcast([P, CHUNK]), func=COPY)
+
+        a, b = scores
+        work = sb.tile([P, 4 * CHUNK], F32, name="work")
+        for c in range(I // CHUNK):
+            cols = slice(c * CHUNK // 16, (c + 1) * CHUNK // 16)
+            from_a = work[:, c * CHUNK : (c + 2) * CHUNK]
+            from_b = sb.tile([P, 2 * CHUNK], F32, name="from_b%d" % c)
+            if c == 0:
+                larger = work[:, 2 * CHUNK : 4 * CHUNK]
+                nc.scalar.activation(out=from_a[:, :CHUNK], in_=a[:].indirect(list1[:, cols]), func=COPY)
+                nc.scalar.activation(out=from_a[:, CHUNK:], in_=a[:].indirect(list2[:, cols]), func=COPY)
+                nc.scalar.activation(out=from_b[:, :CHUNK], in_=b[:].indirect(list2[:, cols]), func=COPY)
+                nc.vector.tensor_copy(out=from_b[:, CHUNK:], in_=b[:].indirect(list1[:, cols]))
+            else:
+                larger = sb.tile([P, 2 * CHUNK], F32, name="larger1")[:]
+                nc.scalar.activation(out=from_b[:, :CHUNK], in_=b[:].indirect(list2[:, cols]), func=COPY)
+                nc.scalar.activation(out=from_b[:, CHUNK:], in_=b[:].indirect(list1[:, cols]), func=COPY)
+                nc.scalar.activation(out=from_a[:, :CHUNK], in_=a[:].indirect(list1[:, cols]), func=COPY)
+                nc.scalar.activation(out=from_a[:, CHUNK:], in_=a[:].indirect(list2[:, cols]), func=COPY)
+            diff = sb.tile([P, CHUNK], F32, name="diff%d" % c)
+            half = CHUNK // 2
+            for h in range(2):
+                part = lambda t: t.rearrange("p (u i) -> p u i", u=2)[:, :, h * half : (h + 1) * half]
+                nc.vector.tensor_tensor(out=part(larger), in0=part(from_a), in1=part(from_b[:]), op=ALU.max)
+            for h in range(2):
+                nc.vector.tensor_tensor(out=diff[:, h * half : (h + 1) * half], in0=larger[:, h * half : (h + 1) * half], in1=larger[:, CHUNK + h * half : CHUNK + (h + 1) * half], op=ALU.subtract)
+            nc.vector.tensor_tensor(out=placed[:].indirect(list3[:, cols]), in0=diff[:], in1=lam_wide[:], op=ALU.mult)
+
+        for n in range(T // STORE):
+            cols = slice(n * STORE, (n + 1) * STORE)
+            total = sb.tile([P, STORE], F32, name="total%d" % n)
+            nc.vector.tensor_tensor(out=total[:], in0=placed[:, cols], in1=stage[:, cols], op=ALU.add)
+            queue = nc.sync if n % 2 == 0 else nc.scalar
+            queue.dma_start(out=out[:, cols], in_=total[:])

@@ -18,9 +18,10 @@ COPY = mybir.ActivationFunctionType.Copy
 
 P = 128
 PACK = 4
-PIECE = 256
 CHUNK = 256
 STORE = 256
+PIECES = ((256, 256, 256, 256), (256, 256, 256, 128, 128))
+BANKS = 8
 
 
 def tile_attend_exchanged_lean_putold_heads_kernel(tc, query, query2, keys_words, keys_scales, lam, old, offs, offs2, offs3, out):
@@ -39,49 +40,58 @@ def tile_attend_exchanged_lean_putold_heads_kernel(tc, query, query2, keys_words
         placed = sb.tile([P, T], F32, name="placed")
 
         nc.vector.memset(placed[:], 0.0)
-        words_hbm = keys_words[0].bitcast(I32)
         scales_hbm = keys_scales[0].bitcast(I32)
         nc.sync.dma_start(out=stage[:, 0:512], in_=query.rearrange("(p j) q -> p (j q)", j=PACK))
-        nc.scalar.dma_start(out=lam_col[:], in_=lam)
+        nc.sync.dma_start(out=words[:].bitcast(I32), in_=keys_words[0].bitcast(I32))
         for quad in range(4):
             nc.sync.dma_start(out=kscale[32 * quad : 32 * quad + 4, :].bitcast(I32), in_=scales_hbm[4 * quad : 4 * quad + 4, :])
-        nc.sync.dma_start(out=words[:].bitcast(I32), in_=words_hbm)
         nc.sync.dma_start(out=stage[:, 512:1024], in_=query2.rearrange("(p j) q -> p (j q)", j=PACK))
         nc.sync.dma_start(list1[:], offs)
         nc.sync.dma_start(list2[:], offs2)
+        nc.sync.dma_start(out=lam_col[:], in_=lam)
         nc.sync.dma_start(list3[:], offs3)
 
         scores = [sb.tile([P, T], F32, name="scores%d" % s) for s in range(2)]
+        used = 0
         for s in range(2):
             grouped = sb.tile([P, Q, PACK], BF16, name="grouped%d" % s, align_bytes=64)
             src = stage[:, 512 * s : 512 * (s + 1)].rearrange("p (j c i) -> p c j i", j=PACK, i=4)
             dst = grouped[:].rearrange("p (c i) j -> p c j i", i=4)
-            nc.vector.tensor_copy(out=dst, in_=src)
+            if s == 0:
+                nc.vector.tensor_copy(out=dst[:, :16], in_=src[:, :16])
+                nc.scalar.copy(out=dst[:, 16:], in_=src[:, 16:])
+            else:
+                nc.vector.tensor_copy(out=dst, in_=src)
             codes = sb.tile([P, Q], U32, name="codes%d" % s, align_bytes=64)
             qscale = sb.tile([P, Q], U8, name="qscale%d" % s, align_bytes=64)
             nc.vector.quantize_mx(out=codes[:].bitcast(FP8X4), scales=qscale[:], in_=grouped[:].rearrange("p q j -> p (q j)"))
-            for n in range(T // PIECE):
-                bank = ps.tile([P, PIECE], F32, name="bank%d_%d" % (s, n))
+            lo = 0
+            for width in PIECES[s]:
+                hi = lo + width
+                bank = ps.tile([P, 512], F32, name="bank%d" % (used % BANKS))
+                used = used + 1
                 nc.tensor.matmul_mx(
-                    out=bank[:],
+                    out=bank[:, :width],
                     lhsT=codes[:].bitcast(FP8X4),
                     lhsT_scale=qscale[:],
-                    rhs=words[:, 2 * n * PIECE : 2 * (n + 1) * PIECE].bitcast(FP4X4),
-                    rhs_scale=kscale[:, n * PIECE : (n + 1) * PIECE],
+                    rhs=words[:, 2 * lo : 2 * hi].bitcast(FP4X4),
+                    rhs_scale=kscale[:, lo:hi],
                     start=True,
                     stop=True,
                 )
                 if s == 0:
-                    nc.scalar.activation(out=scores[s][:, n * PIECE : (n + 1) * PIECE], in_=bank[:], func=COPY)
+                    nc.scalar.activation(out=scores[s][:, lo:hi], in_=bank[:, :width], func=COPY)
                 else:
-                    nc.vector.tensor_copy(out=scores[s][:, n * PIECE : (n + 1) * PIECE], in_=bank[:])
+                    nc.vector.tensor_copy(out=scores[s][:, lo:hi], in_=bank[:, :width])
+                lo = hi
 
         nc.sync.dma_start(out=stage[:], in_=old)
-        lam_wide = sb.tile([P, CHUNK], F32, name="lam_wide")
-        nc.scalar.activation(out=lam_wide[:], in_=lam_col[:, 0:1].to_broadcast([P, CHUNK]), func=COPY)
+        lam_wide = sb.tile([P, CHUNK], F32, name="grouped1", align_bytes=64)
+        nc.gpsimd.tensor_scalar(out=lam_wide[:], in0=lam_col[:, 0:1].to_broadcast([P, CHUNK]), scalar1=1.0, scalar2=0.0, op0=ALU.mult, op1=ALU.add)
 
         a, b = scores
         work = sb.tile([P, 4 * CHUNK], F32, name="work")
+        half = CHUNK // 2
         for c in range(I // CHUNK):
             cols = slice(c * CHUNK // 16, (c + 1) * CHUNK // 16)
             from_a = work[:, c * CHUNK : (c + 2) * CHUNK]
@@ -99,7 +109,6 @@ def tile_attend_exchanged_lean_putold_heads_kernel(tc, query, query2, keys_words
                 nc.scalar.activation(out=from_a[:, :CHUNK], in_=a[:].indirect(list1[:, cols]), func=COPY)
                 nc.scalar.activation(out=from_a[:, CHUNK:], in_=a[:].indirect(list2[:, cols]), func=COPY)
             diff = sb.tile([P, CHUNK], F32, name="diff%d" % c)
-            half = CHUNK // 2
             for h in range(2):
                 part = lambda t: t.rearrange("p (u i) -> p u i", u=2)[:, :, h * half : (h + 1) * half]
                 nc.vector.tensor_tensor(out=part(larger), in0=part(from_a), in1=part(from_b[:]), op=ALU.max)

from contextlib import ExitStack

import concourse.mybir as mybir

D, T, I, Q = 512, 1024, 512, 128
FLOPS = 2 * 2 * D * T * Q

F32 = mybir.dt.float32
BF16 = mybir.dt.bfloat16
I32 = mybir.dt.int32
U32 = mybir.dt.uint32
U16 = mybir.dt.uint16
U8 = mybir.dt.uint8
FP8X4 = mybir.dt.float8_e4m3fn_x4
FP4X4 = mybir.dt.float4_e2m1fn_x4
ALU = mybir.AluOpType
COPY = mybir.ActivationFunctionType.Copy

P = 128
PACK = 4
CHUNK = 256
STORE = 256
PIECES = ((256, 256, 256, 256), (256, 256, 256, 128, 128))
BANKS = 8


def tile_attend_exchanged_lean_putold_heads_kernel(tc, query, query2, keys_words, keys_scales, lam, old, offs, offs2, offs3, out):
    nc = tc.nc
    with ExitStack() as ctx:
        sb = ctx.enter_context(tc.tile_pool(name="sb", bufs=1))
        ps = ctx.enter_context(tc.psum_pool(name="ps", bufs=1))

        list1 = sb.tile([P, I // 16], U16, name="list1")
        list2 = sb.tile([P, I // 16], U16, name="list2")
        list3 = sb.tile([P, I // 16], U16, name="list3")
        stage = sb.tile([P, T], F32, name="stage")
        words = sb.tile([P, 2 * T], U8, name="words", align_bytes=64)
        kscale = sb.tile([P, T], U8, name="kscale", align_bytes=64)
        lam_col = sb.tile([P, 1], F32, name="lam_col")
        placed = sb.tile([P, T], F32, name="placed")

        nc.vector.memset(placed[:], 0.0)
        scales_hbm = keys_scales[0].bitcast(I32)
        nc.sync.dma_start(out=stage[:, 0:512], in_=query.rearrange("(p j) q -> p (j q)", j=PACK))
        nc.sync.dma_start(out=words[:].bitcast(I32), in_=keys_words[0].bitcast(I32))
        for quad in range(4):
            nc.sync.dma_start(out=kscale[32 * quad : 32 * quad + 4, :].bitcast(I32), in_=scales_hbm[4 * quad : 4 * quad + 4, :])
        nc.sync.dma_start(out=stage[:, 512:1024], in_=query2.rearrange("(p j) q -> p (j q)", j=PACK))
        nc.sync.dma_start(list1[:], offs)
        nc.sync.dma_start(list2[:], offs2)
        nc.sync.dma_start(out=lam_col[:], in_=lam)
        nc.sync.dma_start(list3[:], offs3)

        scores = [sb.tile([P, T], F32, name="scores%d" % s) for s in range(2)]
        used = 0
        for s in range(2):
            grouped = sb.tile([P, Q, PACK], BF16, name="grouped%d" % s, align_bytes=64)
            src = stage[:, 512 * s : 512 * (s + 1)].rearrange("p (j c i) -> p c j i", j=PACK, i=4)
            dst = grouped[:].rearrange("p (c i) j -> p c j i", i=4)
            if s == 0:
                nc.vector.tensor_copy(out=dst[:, :16], in_=src[:, :16])
                nc.scalar.copy(out=dst[:, 16:], in_=src[:, 16:])
            else:
                nc.vector.tensor_copy(out=dst, in_=src)
            codes = sb.tile([P, Q], U32, name="codes%d" % s, align_bytes=64)
            qscale = sb.tile([P, Q], U8, name="qscale%d" % s, align_bytes=64)
            nc.vector.quantize_mx(out=codes[:].bitcast(FP8X4), scales=qscale[:], in_=grouped[:].rearrange("p q j -> p (q j)"))
            lo = 0
            for width in PIECES[s]:
                hi = lo + width
                bank = ps.tile([P, 512], F32, name="bank%d" % (used % BANKS))
                used = used + 1
                nc.tensor.matmul_mx(
                    out=bank[:, :width],
                    lhsT=codes[:].bitcast(FP8X4),
                    lhsT_scale=qscale[:],
                    rhs=words[:, 2 * lo : 2 * hi].bitcast(FP4X4),
                    rhs_scale=kscale[:, lo:hi],
                    start=True,
                    stop=True,
                )
                if s == 0:
                    nc.scalar.activation(out=scores[s][:, lo:hi], in_=bank[:, :width], func=COPY)
                else:
                    nc.vector.tensor_copy(out=scores[s][:, lo:hi], in_=bank[:, :width])
                lo = hi

        nc.sync.dma_start(out=stage[:], in_=old)
        lam_wide = sb.tile([P, CHUNK], F32, name="grouped1", align_bytes=64)
        nc.gpsimd.tensor_scalar(out=lam_wide[:], in0=lam_col[:, 0:1].to_broadcast([P, CHUNK]), scalar1=1.0, scalar2=0.0, op0=ALU.mult, op1=ALU.add)

        a, b = scores
        work = sb.tile([P, 4 * CHUNK], F32, name="work")
        half = CHUNK // 2
        for c in range(I // CHUNK):
            cols = slice(c * CHUNK // 16, (c + 1) * CHUNK // 16)
            from_a = work[:, c * CHUNK : (c + 2) * CHUNK]
            from_b = sb.tile([P, 2 * CHUNK], F32, name="from_b%d" % c)
            if c == 0:
                larger = work[:, 2 * CHUNK : 4 * CHUNK]
                nc.scalar.activation(out=from_a[:, :CHUNK], in_=a[:].indirect(list1[:, cols]), func=COPY)
                nc.scalar.activation(out=from_a[:, CHUNK:], in_=a[:].indirect(list2[:, cols]), func=COPY)
                nc.scalar.activation(out=from_b[:, :CHUNK], in_=b[:].indirect(list2[:, cols]), func=COPY)
                nc.vector.tensor_copy(out=from_b[:, CHUNK:], in_=b[:].indirect(list1[:, cols]))
            else:
                larger = sb.tile([P, 2 * CHUNK], F32, name="larger1")[:]
                nc.scalar.activation(out=from_b[:, :CHUNK], in_=b[:].indirect(list2[:, cols]), func=COPY)
                nc.scalar.activation(out=from_b[:, CHUNK:], in_=b[:].indirect(list1[:, cols]), func=COPY)
                nc.scalar.activation(out=from_a[:, :CHUNK], in_=a[:].indirect(list1[:, cols]), func=COPY)
                nc.scalar.activation(out=from_a[:, CHUNK:], in_=a[:].indirect(list2[:, cols]), func=COPY)
            diff = sb.tile([P, CHUNK], F32, name="diff%d" % c)
            for h in range(2):
                part = lambda t: t.rearrange("p (u i) -> p u i", u=2)[:, :, h * half : (h + 1) * half]
                nc.vector.tensor_tensor(out=part(larger), in0=part(from_a), in1=part(from_b[:]), op=ALU.max)
            for h in range(2):
                nc.vector.tensor_tensor(out=diff[:, h * half : (h + 1) * half], in0=larger[:, h * half : (h + 1) * half], in1=larger[:, CHUNK + h * half : CHUNK + (h + 1) * half], op=ALU.subtract)
            nc.vector.tensor_tensor(out=placed[:].indirect(list3[:, cols]), in0=diff[:], in1=lam_wide[:], op=ALU.mult)

        for n in range(T // STORE):
            cols = slice(n * STORE, (n + 1) * STORE)
            total = sb.tile([P, STORE], F32, name="total%d" % n)
            nc.vector.tensor_tensor(out=total[:], in0=placed[:, cols], in1=stage[:, cols], op=ALU.add)
            queue = nc.sync if n % 2 == 0 else nc.scalar
            queue.dma_start(out=out[:, cols], in_=total[:])
